import numpy as np
import ml_dtypes


def mxq(x, axis, fmt="e4m3"):
    dtype, down = {"e4m3": (ml_dtypes.float8_e4m3fn, 7), "e5m2": (ml_dtypes.float8_e5m2, 14)}[fmt]
    v = np.moveaxis(np.asarray(x, np.float32).astype(ml_dtypes.bfloat16).astype(np.float64), axis, -1)
    blocks = v.reshape(v.shape[:-1] + (-1, 32))
    amax = np.abs(blocks).max(-1, keepdims=True)
    byte = np.maximum(np.where(amax > 0, np.frexp(amax)[1] - 1 + 127, 0) - down, 1)
    scale = np.exp2(byte - 127.0)
    codes = (blocks / scale).astype(np.float32).astype(dtype).astype(np.float64)
    return np.moveaxis((codes * scale).reshape(v.shape), -1, axis)


WIDE = False


def mx_kscale(k):
    if not WIDE:
        return np.ones(k)
    levels = np.array([30, -30])
    if k % 512:
        return np.exp2(np.random.permutation(np.resize(levels, k // 32))).repeat(32)
    a = np.empty((k // 512, 16))
    for p in range(k // 512):
        a[p, :8] = np.random.permutation(np.resize(levels, 8))
        for g in range(8):
            far = levels[np.abs(levels - a[p, g]) >= 10]
            a[p, g + 8] = far[np.random.randint(len(far))]
    return np.exp2(a.ravel()).repeat(32)


def f64(x):
    return np.asarray(x).astype(np.float64)


def striped(idx):
    return np.tile(np.asarray(idx).reshape(-1, 16).T, (8, 1)).astype(np.uint16)


def unstriped(offs):
    return offs[:16].T.reshape(-1).astype(np.int64)


E2M1 = np.array([0.0, 0.5, 1.0, 1.5, 2.0, 3.0, 4.0, 6.0, -0.0, -0.5, -1.0, -1.5, -2.0, -3.0, -4.0, -6.0])


def pack_weight(w, fmt):
    k, n = w.shape
    w = f64(np.asarray(w, np.float32).astype(ml_dtypes.bfloat16)).reshape(k // 32, 32, n)
    amax = np.abs(w).max(1)
    if fmt == "e4m3":
        byte = np.frexp(amax)[1] - 1 + 127 - 7
    else:
        mant, ex = np.frexp(amax / 6.0)
        byte = np.where(mant > 0.5, ex, ex - 1) + 127
    byte = np.clip(np.where(amax > 0, byte, 1), 1, 254)
    scaled = (w * np.exp2(127.0 - byte)[:, None, :]).reshape(k, n).astype(np.float32)
    by_word = np.ascontiguousarray(scaled.reshape(k // 512, 128, 4, n).transpose(0, 1, 3, 2))
    if fmt == "e4m3":
        words = by_word.astype(ml_dtypes.float8_e4m3fn).view(np.uint8)
    else:
        c = by_word.astype(ml_dtypes.float4_e2m1fn).view(np.uint8) & 0xF
        words = (c[..., 0::2] | (c[..., 1::2] << 4)).reshape(k // 512, 128, 2 * n)
    return np.ascontiguousarray(words), np.ascontiguousarray(byte.astype(np.uint8).reshape(k // 512, 16, n))


def unpack_weight(words, scales, fmt):
    g, _, n = scales.shape
    words = np.ascontiguousarray(words).reshape(g, 128, n, -1)
    if fmt == "e4m3":
        vals = words.view(ml_dtypes.float8_e4m3fn).astype(np.float64)
    else:
        nib = np.empty((g, 128, n, 4), np.uint8)
        nib[..., 0::2] = words & 0xF
        nib[..., 1::2] = words >> 4
        vals = E2M1[nib]
    vals = vals * np.repeat(np.exp2(scales.astype(np.float64) - 127.0), 8, axis=1)[..., None]
    return vals.transpose(0, 1, 3, 2).reshape(g * 512, n)


K, T, J, I, M = 1024, 1024, 256, 256, 128


def setup_inputs():
    n = np.random.standard_normal
    idx = np.random.permutation(T)[:J]
    idx2 = np.random.permutation(I)[:M]
    fk = mx_kscale(K)
    xtp = pack_weight(n((K, T)) * 0.04 * fk[:, None], "e2m1")
    return {
        "xt_words": xtp[0],
        "xt_scales": xtp[1],
        "ky": (n((K, I)) / fk[:, None]).astype(np.float32),
        "bi": (np.random.uniform(-0.7, 0.7, (1, I))).astype(np.float32),
        "rs": (1.0 * n((J, M))).astype(np.float32),
        "offs": striped(idx),
        "offs2": striped(idx2),
    }


def reference(xt_words, xt_scales, ky, bi, rs, offs, offs2):
    idx = unstriped(offs)
    idx2 = unstriped(offs2)
    xtu = unpack_weight(xt_words, xt_scales, "e2m1")
    xtidxg = xtu[:, idx]
    kyq = mxq(f64(ky), 0, "e5m2")
    a0 = xtidxg.T @ kyq
    a = a0 + f64(bi)
    mn = np.mean(np.abs(a), axis=1, keepdims=True)
    y = a[:, idx2] / mn + 0.5 * f64(rs)
    return y

@@ -1,0 +1,122 @@
+from contextlib import ExitStack
+
+import concourse.mybir as mybir
+
+K, T, J, I, M = 1024, 1024, 256, 256, 128
+FLOPS = 2 * K * J * I
+
+F32 = mybir.dt.float32
+BF16 = mybir.dt.bfloat16
+I32 = mybir.dt.int32
+U32 = mybir.dt.uint32
+U16 = mybir.dt.uint16
+U8 = mybir.dt.uint8
+E5M2X4 = mybir.dt.float8_e5m2_x4
+E2M1X4 = mybir.dt.float4_e2m1fn_x4
+ALU = mybir.AluOpType
+ACT = mybir.ActivationFunctionType
+
+P = 128
+PACK = 4
+K_PASS = P * PACK
+PASSES = K // K_PASS
+ROW_TILES = J // P
+LIST_COLS = P // 16
+SCALAR_COLS = 128
+
+
+def round_and_interleave(copy, grouped, raw, cols):
+    copy(
+        out=grouped[:, cols, :].rearrange("p (c i) t -> p c t i", i=4),
+        in_=raw[:, :, cols].rearrange("p t (c i) -> p c t i", i=4),
+    )
+
+
+def tile_list_scores_picked_given_looked_kernel(tc, xt_words, xt_scales, ky, bi, rs, offs, offs2, out):
+    nc = tc.nc
+    with ExitStack() as ctx:
+        pool = ctx.enter_context(tc.tile_pool(name="sbuf", bufs=1))
+        psum = ctx.enter_context(tc.psum_pool(name="psum", bufs=1))
+
+        token_list = pool.tile([P, J // 16], U16, name="token_list")
+        column_list = pool.tile([P, M // 16], U16, name="column_list")
+        all_scales = pool.tile([P, PASSES, T], U8, name="all_scales", align_bytes=64)
+        all_words = [pool.tile([P, T], U16, name="all_words%d" % z, align_bytes=64) for z in range(PASSES)]
+        ky_raw = [pool.tile([P, PACK, I], F32, name="ky_raw%d" % z, align_bytes=64) for z in range(PASSES)]
+        bias = pool.tile([P, I], F32, name="bias", align_bytes=64)
+        resid = pool.tile([P, ROW_TILES, M], F32, name="resid", align_bytes=64)
+
+        nc.gpsimd.memset(all_scales[:].rearrange("p z c -> p (z c)").bitcast(I32), 0)
+
+        nc.sync.dma_start(token_list[:], offs)
+        for q in range(4):
+            nc.sync.dma_start(
+                all_scales[32 * q : 32 * q + 4, :, :].bitcast(I32),
+                xt_scales[:, 4 * q : 4 * q + 4, :].rearrange("z r c -> r z c").bitcast(I32),
+            )
+        for z in range(PASSES):
+            nc.sync.dma_start(ky_raw[z][:], ky[z * K_PASS : (z + 1) * K_PASS, :].rearrange("(p t) i -> p t i", t=PACK))
+        for z in range(PASSES):
+            nc.sync.dma_start(all_words[z][:].bitcast(I32), xt_words[z].bitcast(I32))
+        nc.sync.dma_start(bias[:], bi.partition_broadcast(P))
+        nc.sync.dma_start(column_list[:], offs2)
+        nc.sync.dma_start(resid[:], rs.rearrange("(r p) m -> p r m", p=P))
+
+        x_scales = []
+        for z in range(PASSES):
+            picked = pool.tile([P, J], U8, name="x_scales%d" % z, align_bytes=64)
+            nc.vector.tensor_copy(picked[:], all_scales[:, z, :].indirect(token_list[:]))
+            x_scales.append(picked)
+
+        k_codes, k_scales = [], []
+        for z in range(PASSES):
+            grouped = pool.tile([P, I, PACK], BF16, name="grouped%d" % z, align_bytes=64)
+            round_and_interleave(nc.scalar.copy, grouped, ky_raw[z], slice(0, SCALAR_COLS))
+            round_and_interleave(nc.vector.tensor_copy, grouped, ky_raw[z], slice(SCALAR_COLS, I))
+            codes = pool.tile([P, I], U32, name="k_codes%d" % z, align_bytes=64)
+            scales = pool.tile([P, I], U8, name="k_scales%d" % z, align_bytes=64)
+            nc.vector.quantize_mx(
+                out=codes[:].bitcast(E5M2X4), scales=scales[:], in_=grouped[:].rearrange("p c t -> p (c t)")
+            )
+            k_codes.append(codes)
+            k_scales.append(scales)
+
+        acc = [psum.tile([P, I], F32, name="acc%d" % r) for r in range(ROW_TILES)]
+        for z in range(PASSES):
+            for r in range(ROW_TILES):
+                x_words = pool.tile([P, P], U16, name="x_words%d_%d" % (z, r), align_bytes=64)
+                entries = token_list[:, r * LIST_COLS : (r + 1) * LIST_COLS]
+                nc.vector.tensor_copy(x_words[:], all_words[z][:].indirect(entries))
+                nc.tensor.matmul_mx(
+                    out=acc[r][:],
+                    lhsT=x_words[:].bitcast(E2M1X4),
+                    lhsT_scale=x_scales[z][:, r * P : (r + 1) * P],
+                    rhs=k_codes[z][:].bitcast(E5M2X4),
+                    rhs_scale=k_scales[z][:],
+                    start=(z == 0),
+                    stop=(z == PASSES - 1),
+                )
+
+        half_resid = pool.tile([P, ROW_TILES, M], F32, name="half_resid", align_bytes=64)
+        nc.scalar.activation(half_resid[:], resid[:], ACT.Copy, scale=0.5)
+
+        scores, means = [], []
+        for r in range(ROW_TILES):
+            a = pool.tile([P, I], F32, name="scores%d" % r, align_bytes=64)
+            nc.vector.tensor_tensor(a[:], acc[r][:], bias[:], ALU.add)
+            magnitude = pool.tile([P, I], F32, name="magnitude%d" % r, align_bytes=64)
+            mean = pool.tile([P, 1], F32, name="mean%d" % r)
+            nc.scalar.activation(magnitude[:], a[:], ACT.Abs, scale=1.0 / I, accum_out=mean[:])
+            scores.append(a)
+            means.append(mean)
+
+        for r in range(ROW_TILES):
+            looked_up = pool.tile([P, M], F32, name="looked_up%d" % r, align_bytes=64)
+            nc.vector.tensor_copy(looked_up[:], scores[r][:].indirect(column_list[:]))
+            inv_mean = pool.tile([P, 1], F32, name="inv_mean%d" % r)
+            nc.vector.reciprocal(inv_mean[:], means[r][:])
+            result = pool.tile([P, M], F32, name="result%d" % r, align_bytes=64)
+            nc.vector.scalar_tensor_tensor(
+                result[:], looked_up[:], inv_mean[:], half_resid[:, r, :], ALU.mult, ALU.add
+            )
+            nc.sync.dma_start(out[r * P : (r + 1) * P, :], result[:])

@@ -1,6 +1,7 @@
 from contextlib import ExitStack
 
 import concourse.mybir as mybir
+from concourse.masks import make_identity
 
 K, T, J, I, M = 1024, 1024, 256, 256, 128
 FLOPS = 2 * K * J * I
@@ -22,7 +23,7 @@ K_PASS = P * PACK
 PASSES = K // K_PASS
 ROW_TILES = J // P
 LIST_COLS = P // 16
-SCALAR_COLS = 128
+SCALAR_COLS = (96, 128)
 
 
 def round_and_interleave(copy, grouped, raw, cols):
@@ -42,37 +43,46 @@ def tile_list_scores_picked_given_looked_kernel(tc, xt_words, xt_scales, ky, bi,
         column_list = pool.tile([P, M // 16], U16, name="column_list")
         all_scales = pool.tile([P, PASSES, T], U8, name="all_scales", align_bytes=64)
         all_words = [pool.tile([P, T], U16, name="all_words%d" % z, align_bytes=64) for z in range(PASSES)]
-        ky_raw = [pool.tile([P, PACK, I], F32, name="ky_raw%d" % z, align_bytes=64) for z in range(PASSES)]
+        ky_raw = [pool.tile([P, PACK, I], F32, name="ky_raw%d" % z, tag="ky_raw%d" % z, align_bytes=64) for z in range(PASSES)]
         bias = pool.tile([P, I], F32, name="bias", align_bytes=64)
         resid = pool.tile([P, ROW_TILES, M], F32, name="resid", align_bytes=64)
 
-        nc.gpsimd.memset(all_scales[:].rearrange("p z c -> p (z c)").bitcast(I32), 0)
+        nc.vector.memset(all_scales[:, 0, :].bitcast(I32), 0)
+        nc.gpsimd.memset(all_scales[:, 1, :].bitcast(I32), 0)
 
+        def load_keys(z):
+            nc.sync.dma_start(ky_raw[z][:], ky[z * K_PASS : (z + 1) * K_PASS, :].rearrange("(p t) i -> p t i", t=PACK))
+
+        bias_pairs = pool.tile([P, 2], F32, name="bias_pairs")
+        nc.scalar.dma_start(bias_pairs[:], bi.rearrange("o (p c) -> (o p) c", c=2))
         nc.sync.dma_start(token_list[:], offs)
+        nc.sync.dma_start(all_words[0][:].bitcast(I32), xt_words[0].bitcast(I32))
+        load_keys(0)
+        nc.sync.dma_start(column_list[:], offs2)
         for q in range(4):
             nc.sync.dma_start(
                 all_scales[32 * q : 32 * q + 4, :, :].bitcast(I32),
                 xt_scales[:, 4 * q : 4 * q + 4, :].rearrange("z r c -> r z c").bitcast(I32),
             )
-        for z in range(PASSES):
-            nc.sync.dma_start(ky_raw[z][:], ky[z * K_PASS : (z + 1) * K_PASS, :].rearrange("(p t) i -> p t i", t=PACK))
-        for z in range(PASSES):
-            nc.sync.dma_start(all_words[z][:].bitcast(I32), xt_words[z].bitcast(I32))
-        nc.sync.dma_start(bias[:], bi.partition_broadcast(P))
-        nc.sync.dma_start(column_list[:], offs2)
+        load_keys(1)
+        nc.sync.dma_start(all_words[1][:].bitcast(I32), xt_words[1].bitcast(I32))
         nc.sync.dma_start(resid[:], rs.rearrange("(r p) m -> p r m", p=P))
 
-        x_scales = []
-        for z in range(PASSES):
-            picked = pool.tile([P, J], U8, name="x_scales%d" % z, align_bytes=64)
-            nc.vector.tensor_copy(picked[:], all_scales[:, z, :].indirect(token_list[:]))
-            x_scales.append(picked)
+        identity = pool.tile([P, P], F32, name="identity", align_bytes=64)
+        make_identity(nc, identity[:])
+        bias_spread = psum.tile([P, 2, P], F32, name="bias_spread")
+        for c in range(2):
+            nc.tensor.transpose(bias_spread[:, c, :], bias_pairs[:, c : c + 1].to_broadcast([P, P]), identity[:])
+        nc.scalar.copy(bias[:].rearrange("p (n c) -> p n c", c=2), bias_spread[:].rearrange("p c n -> p n c"))
 
-        k_codes, k_scales = [], []
+        first_words = pool.tile([P, J], U16, name="first_words", align_bytes=64)
+        nc.vector.tensor_copy(first_words[:], all_words[0][:].indirect(token_list[:]))
+
+        k_codes, k_scales, x_scales = [], [], []
         for z in range(PASSES):
             grouped = pool.tile([P, I, PACK], BF16, name="grouped%d" % z, align_bytes=64)
-            round_and_interleave(nc.scalar.copy, grouped, ky_raw[z], slice(0, SCALAR_COLS))
-            round_and_interleave(nc.vector.tensor_copy, grouped, ky_raw[z], slice(SCALAR_COLS, I))
+            round_and_interleave(nc.scalar.copy, grouped, ky_raw[z], slice(0, SCALAR_COLS[z]))
+            round_and_interleave(nc.vector.tensor_copy, grouped, ky_raw[z], slice(SCALAR_COLS[z], I))
             codes = pool.tile([P, I], U32, name="k_codes%d" % z, align_bytes=64)
             scales = pool.tile([P, I], U8, name="k_scales%d" % z, align_bytes=64)
             nc.vector.quantize_mx(
@@ -80,16 +90,25 @@ def tile_list_scores_picked_given_looked_kernel(tc, xt_words, xt_scales, ky, bi,
             )
             k_codes.append(codes)
             k_scales.append(scales)
+            if z == 0:
+                for y in range(PASSES):
+                    picked = pool.tile([P, J], U8, name="x_scales%d" % y, align_bytes=64)
+                    nc.vector.tensor_copy(picked[:], all_scales[:, y, :].indirect(token_list[:]))
+                    x_scales.append(picked)
 
         acc = [psum.tile([P, I], F32, name="acc%d" % r) for r in range(ROW_TILES)]
+        last_words = pool.tile([P, J], U16, name="last_words", tag="ky_raw1", align_bytes=64)
         for z in range(PASSES):
             for r in range(ROW_TILES):
-                x_words = pool.tile([P, P], U16, name="x_words%d_%d" % (z, r), align_bytes=64)
-                entries = token_list[:, r * LIST_COLS : (r + 1) * LIST_COLS]
-                nc.vector.tensor_copy(x_words[:], all_words[z][:].indirect(entries))
+                if z == 0:
+                    x_words = first_words[:, r * P : (r + 1) * P]
+                else:
+                    entries = token_list[:, r * LIST_COLS : (r + 1) * LIST_COLS]
+                    x_words = last_words[:, r * P : (r + 1) * P]
+                    nc.vector.tensor_copy(x_words, all_words[z][:].indirect(entries))
                 nc.tensor.matmul_mx(
                     out=acc[r][:],
-                    lhsT=x_words[:].bitcast(E2M1X4),
+                    lhsT=x_words.bitcast(E2M1X4),
                     lhsT_scale=x_scales[z][:, r * P : (r + 1) * P],
                     rhs=k_codes[z][:].bitcast(E5M2X4),
                     rhs_scale=k_scales[z][:],
@@ -110,13 +129,18 @@ def tile_list_scores_picked_given_looked_kernel(tc, xt_words, xt_scales, ky, bi,
             scores.append(a)
             means.append(mean)
 
+        looked_up, inv_means = [], []
         for r in range(ROW_TILES):
-            looked_up = pool.tile([P, M], F32, name="looked_up%d" % r, align_bytes=64)
-            nc.vector.tensor_copy(looked_up[:], scores[r][:].indirect(column_list[:]))
+            picked = pool.tile([P, M], F32, name="looked_up%d" % r, align_bytes=64)
+            nc.vector.tensor_copy(picked[:], scores[r][:].indirect(column_list[:]))
             inv_mean = pool.tile([P, 1], F32, name="inv_mean%d" % r)
             nc.vector.reciprocal(inv_mean[:], means[r][:])
+            looked_up.append(picked)
+            inv_means.append(inv_mean)
+
+        for r, queue in enumerate((nc.scalar, nc.sync)):
             result = pool.tile([P, M], F32, name="result%d" % r, align_bytes=64)
             nc.vector.scalar_tensor_tensor(
-                result[:], looked_up[:], inv_mean[:], half_resid[:, r, :], ALU.mult, ALU.add
+                result[:], looked_up[r][:], inv_means[r][:], half_resid[:, r, :], ALU.mult, ALU.add
             )
-            nc.sync.dma_start(out[r * P : (r + 1) * P, :], result[:])
+            queue.dma_start(out[r * P : (r + 1) * P, :], result[:])

@@ -23,7 +23,7 @@ K_PASS = P * PACK
 PASSES = K // K_PASS
 ROW_TILES = J // P
 LIST_COLS = P // 16
-SCALAR_COLS = (96, 128)
+SCALAR_COLS = (184, 112)
 
 
 def round_and_interleave(copy, grouped, raw, cols):
@@ -47,25 +47,24 @@ def tile_list_scores_picked_given_looked_kernel(tc, xt_words, xt_scales, ky, bi,
         bias = pool.tile([P, I], F32, name="bias", align_bytes=64)
         resid = pool.tile([P, ROW_TILES, M], F32, name="resid", align_bytes=64)
 
-        nc.vector.memset(all_scales[:, 0, :].bitcast(I32), 0)
-        nc.gpsimd.memset(all_scales[:, 1, :].bitcast(I32), 0)
+        scale_words = all_scales[:].rearrange("p z c -> p (z c)").bitcast(I32)
+        nc.vector.memset(scale_words[:, 0:256], 0)
+        nc.gpsimd.memset(scale_words[:, 256:512], 0)
 
         def load_keys(z):
             nc.sync.dma_start(ky_raw[z][:], ky[z * K_PASS : (z + 1) * K_PASS, :].rearrange("(p t) i -> p t i", t=PACK))
 
-        bias_pairs = pool.tile([P, 2], F32, name="bias_pairs")
-        nc.scalar.dma_start(bias_pairs[:], bi.rearrange("o (p c) -> (o p) c", c=2))
         nc.sync.dma_start(token_list[:], offs)
         nc.sync.dma_start(all_words[0][:].bitcast(I32), xt_words[0].bitcast(I32))
+        bias_pairs = pool.tile([P, 2], F32, name="bias_pairs")
+        nc.sync.dma_start(bias_pairs[:], bi.rearrange("o (p c) -> (o p) c", c=2))
+        scale_rows = xt_scales.rearrange("z (q r) c -> r q z c", r=4)
+        for r in range(4):
+            nc.sync.dma_start(all_scales[r:P:32, :, :].bitcast(I32), scale_rows[r].bitcast(I32))
         load_keys(0)
-        nc.sync.dma_start(column_list[:], offs2)
-        for q in range(4):
-            nc.sync.dma_start(
-                all_scales[32 * q : 32 * q + 4, :, :].bitcast(I32),
-                xt_scales[:, 4 * q : 4 * q + 4, :].rearrange("z r c -> r z c").bitcast(I32),
-            )
         load_keys(1)
         nc.sync.dma_start(all_words[1][:].bitcast(I32), xt_words[1].bitcast(I32))
+        nc.sync.dma_start(column_list[:], offs2)
         nc.sync.dma_start(resid[:], rs.rearrange("(r p) m -> p r m", p=P))
 
         identity = pool.tile([P, P], F32, name="identity", align_bytes=64)
@@ -78,7 +77,13 @@ def tile_list_scores_picked_given_looked_kernel(tc, xt_words, xt_scales, ky, bi,
         first_words = pool.tile([P, J], U16, name="first_words", align_bytes=64)
         nc.vector.tensor_copy(first_words[:], all_words[0][:].indirect(token_list[:]))
 
-        k_codes, k_scales, x_scales = [], [], []
+        x_scales = []
+        for z in range(PASSES):
+            picked = pool.tile([P, J], U8, name="x_scales%d" % z, align_bytes=64)
+            nc.vector.tensor_copy(picked[:], all_scales[:, z, :].indirect(token_list[:]))
+            x_scales.append(picked)
+
+        k_codes, k_scales = [], []
         for z in range(PASSES):
             grouped = pool.tile([P, I, PACK], BF16, name="grouped%d" % z, align_bytes=64)
             round_and_interleave(nc.scalar.copy, grouped, ky_raw[z], slice(0, SCALAR_COLS[z]))
@@ -90,11 +95,6 @@ def tile_list_scores_picked_given_looked_kernel(tc, xt_words, xt_scales, ky, bi,
             )
             k_codes.append(codes)
             k_scales.append(scales)
-            if z == 0:
-                for y in range(PASSES):
-                    picked = pool.tile([P, J], U8, name="x_scales%d" % y, align_bytes=64)
-                    nc.vector.tensor_copy(picked[:], all_scales[:, y, :].indirect(token_list[:]))
-                    x_scales.append(picked)
 
         acc = [psum.tile([P, I], F32, name="acc%d" % r) for r in range(ROW_TILES)]
         last_words = pool.tile([P, J], U16, name="last_words", tag="ky_raw1", align_bytes=64)

@@ -23,7 +23,7 @@ K_PASS = P * PACK
 PASSES = K // K_PASS
 ROW_TILES = J // P
 LIST_COLS = P // 16
-SCALAR_COLS = (184, 112)
+SCALAR_COLS = (164, 120)
 
 
 def round_and_interleave(copy, grouped, raw, cols):
@@ -85,7 +85,8 @@ def tile_list_scores_picked_given_looked_kernel(tc, xt_words, xt_scales, ky, bi,
 
         k_codes, k_scales = [], []
         for z in range(PASSES):
-            grouped = pool.tile([P, I, PACK], BF16, name="grouped%d" % z, align_bytes=64)
+            slot = "grouped0" if z == 0 else "ky_raw0"
+            grouped = pool.tile([P, I, PACK], BF16, name="grouped%d" % z, tag=slot, align_bytes=64)
             round_and_interleave(nc.scalar.copy, grouped, ky_raw[z], slice(0, SCALAR_COLS[z]))
             round_and_interleave(nc.vector.tensor_copy, grouped, ky_raw[z], slice(SCALAR_COLS[z], I))
             codes = pool.tile([P, I], U32, name="k_codes%d" % z, align_bytes=64)
@@ -97,14 +98,17 @@ def tile_list_scores_picked_given_looked_kernel(tc, xt_words, xt_scales, ky, bi,
             k_scales.append(scales)
 
         acc = [psum.tile([P, I], F32, name="acc%d" % r) for r in range(ROW_TILES)]
-        last_words = pool.tile([P, J], U16, name="last_words", tag="ky_raw1", align_bytes=64)
+        last_words = [
+            pool.tile([P, P], U16, name="last_words0", tag="grouped0", align_bytes=64),
+            pool.tile([P, P], U16, name="last_words1", tag="ky_raw1", align_bytes=64),
+        ]
         for z in range(PASSES):
             for r in range(ROW_TILES):
                 if z == 0:
                     x_words = first_words[:, r * P : (r + 1) * P]
                 else:
                     entries = token_list[:, r * LIST_COLS : (r + 1) * LIST_COLS]
-                    x_words = last_words[:, r * P : (r + 1) * P]
+                    x_words = last_words[r][:]
                     nc.vector.tensor_copy(x_words, all_words[z][:].indirect(entries))
                 nc.tensor.matmul_mx(
                     out=acc[r][:],
@@ -132,7 +136,10 @@ def tile_list_scores_picked_given_looked_kernel(tc, xt_words, xt_scales, ky, bi,
         looked_up, inv_means = [], []
         for r in range(ROW_TILES):
             picked = pool.tile([P, M], F32, name="looked_up%d" % r, align_bytes=64)
-            nc.vector.tensor_copy(picked[:], scores[r][:].indirect(column_list[:]))
+            if r == 0:
+                nc.vector.tensor_copy(picked[:], scores[r][:].indirect(column_list[:]))
+            else:
+                nc.scalar.activation(picked[:], scores[r][:].indirect(column_list[:]), ACT.Copy)
             inv_mean = pool.tile([P, 1], F32, name="inv_mean%d" % r)
             nc.vector.reciprocal(inv_mean[:], means[r][:])
             looked_up.append(picked)

from contextlib import ExitStack

import concourse.mybir as mybir
from concourse.masks import make_identity

K, T, J, I, M = 1024, 1024, 256, 256, 128
FLOPS = 2 * K * J * I

F32 = mybir.dt.float32
BF16 = mybir.dt.bfloat16
I32 = mybir.dt.int32
U32 = mybir.dt.uint32
U16 = mybir.dt.uint16
U8 = mybir.dt.uint8
E5M2X4 = mybir.dt.float8_e5m2_x4
E2M1X4 = mybir.dt.float4_e2m1fn_x4
ALU = mybir.AluOpType
ACT = mybir.ActivationFunctionType

P = 128
PACK = 4
K_PASS = P * PACK
PASSES = K // K_PASS
ROW_TILES = J // P
LIST_COLS = P // 16
SCALAR_COLS = (164, 120)


def round_and_interleave(copy, grouped, raw, cols):
    copy(
        out=grouped[:, cols, :].rearrange("p (c i) t -> p c t i", i=4),
        in_=raw[:, :, cols].rearrange("p t (c i) -> p c t i", i=4),
    )


def tile_list_scores_picked_given_looked_kernel(tc, xt_words, xt_scales, ky, bi, rs, offs, offs2, out):
    nc = tc.nc
    with ExitStack() as ctx:
        pool = ctx.enter_context(tc.tile_pool(name="sbuf", bufs=1))
        psum = ctx.enter_context(tc.psum_pool(name="psum", bufs=1))

        token_list = pool.tile([P, J // 16], U16, name="token_list")
        column_list = pool.tile([P, M // 16], U16, name="column_list")
        all_scales = pool.tile([P, PASSES, T], U8, name="all_scales", align_bytes=64)
        all_words = [pool.tile([P, T], U16, name="all_words%d" % z, align_bytes=64) for z in range(PASSES)]
        ky_raw = [pool.tile([P, PACK, I], F32, name="ky_raw%d" % z, tag="ky_raw%d" % z, align_bytes=64) for z in range(PASSES)]
        bias = pool.tile([P, I], F32, name="bias", align_bytes=64)
        resid = pool.tile([P, ROW_TILES, M], F32, name="resid", align_bytes=64)

        scale_words = all_scales[:].rearrange("p z c -> p (z c)").bitcast(I32)
        nc.vector.memset(scale_words[:, 0:256], 0)
        nc.gpsimd.memset(scale_words[:, 256:512], 0)

        def load_keys(z):
            nc.sync.dma_start(ky_raw[z][:], ky[z * K_PASS : (z + 1) * K_PASS, :].rearrange("(p t) i -> p t i", t=PACK))

        nc.sync.dma_start(token_list[:], offs)
        nc.sync.dma_start(all_words[0][:].bitcast(I32), xt_words[0].bitcast(I32))
        bias_pairs = pool.tile([P, 2], F32, name="bias_pairs")
        nc.sync.dma_start(bias_pairs[:], bi.rearrange("o (p c) -> (o p) c", c=2))
        scale_rows = xt_scales.rearrange("z (q r) c -> r q z c", r=4)
        for r in range(4):
            nc.sync.dma_start(all_scales[r:P:32, :, :].bitcast(I32), scale_rows[r].bitcast(I32))
        load_keys(0)
        load_keys(1)
        nc.sync.dma_start(all_words[1][:].bitcast(I32), xt_words[1].bitcast(I32))
        nc.sync.dma_start(column_list[:], offs2)
        nc.sync.dma_start(resid[:], rs.rearrange("(r p) m -> p r m", p=P))

        identity = pool.tile([P, P], F32, name="identity", align_bytes=64)
        make_identity(nc, identity[:])
        bias_spread = psum.tile([P, 2, P], F32, name="bias_spread")
        for c in range(2):
            nc.tensor.transpose(bias_spread[:, c, :], bias_pairs[:, c : c + 1].to_broadcast([P, P]), identity[:])
        nc.scalar.copy(bias[:].rearrange("p (n c) -> p n c", c=2), bias_spread[:].rearrange("p c n -> p n c"))

        first_words = pool.tile([P, J], U16, name="first_words", align_bytes=64)
        nc.vector.tensor_copy(first_words[:], all_words[0][:].indirect(token_list[:]))

        x_scales = []
        for z in range(PASSES):
            picked = pool.tile([P, J], U8, name="x_scales%d" % z, align_bytes=64)
            nc.vector.tensor_copy(picked[:], all_scales[:, z, :].indirect(token_list[:]))
            x_scales.append(picked)

        k_codes, k_scales = [], []
        for z in range(PASSES):
            slot = "grouped0" if z == 0 else "ky_raw0"
            grouped = pool.tile([P, I, PACK], BF16, name="grouped%d" % z, tag=slot, align_bytes=64)
            round_and_interleave(nc.scalar.copy, grouped, ky_raw[z], slice(0, SCALAR_COLS[z]))
            round_and_interleave(nc.vector.tensor_copy, grouped, ky_raw[z], slice(SCALAR_COLS[z], I))
            codes = pool.tile([P, I], U32, name="k_codes%d" % z, align_bytes=64)
            scales = pool.tile([P, I], U8, name="k_scales%d" % z, align_bytes=64)
            nc.vector.quantize_mx(
                out=codes[:].bitcast(E5M2X4), scales=scales[:], in_=grouped[:].rearrange("p c t -> p (c t)")
            )
            k_codes.append(codes)
            k_scales.append(scales)

        acc = [psum.tile([P, I], F32, name="acc%d" % r) for r in range(ROW_TILES)]
        last_words = [
            pool.tile([P, P], U16, name="last_words0", tag="grouped0", align_bytes=64),
            pool.tile([P, P], U16, name="last_words1", tag="ky_raw1", align_bytes=64),
        ]
        for z in range(PASSES):
            for r in range(ROW_TILES):
                if z == 0:
                    x_words = first_words[:, r * P : (r + 1) * P]
                else:
                    entries = token_list[:, r * LIST_COLS : (r + 1) * LIST_COLS]
                    x_words = last_words[r][:]
                    nc.vector.tensor_copy(x_words, all_words[z][:].indirect(entries))
                nc.tensor.matmul_mx(
                    out=acc[r][:],
                    lhsT=x_words.bitcast(E2M1X4),
                    lhsT_scale=x_scales[z][:, r * P : (r + 1) * P],
                    rhs=k_codes[z][:].bitcast(E5M2X4),
                    rhs_scale=k_scales[z][:],
                    start=(z == 0),
                    stop=(z == PASSES - 1),
                )

        half_resid = pool.tile([P, ROW_TILES, M], F32, name="half_resid", align_bytes=64)
        nc.scalar.activation(half_resid[:], resid[:], ACT.Copy, scale=0.5)

        scores, means = [], []
        for r in range(ROW_TILES):
            a = pool.tile([P, I], F32, name="scores%d" % r, align_bytes=64)
            nc.vector.tensor_tensor(a[:], acc[r][:], bias[:], ALU.add)
            magnitude = pool.tile([P, I], F32, name="magnitude%d" % r, align_bytes=64)
            mean = pool.tile([P, 1], F32, name="mean%d" % r)
            nc.scalar.activation(magnitude[:], a[:], ACT.Abs, scale=1.0 / I, accum_out=mean[:])
            scores.append(a)
            means.append(mean)

        looked_up, inv_means = [], []
        for r in range(ROW_TILES):
            picked = pool.tile([P, M], F32, name="looked_up%d" % r, align_bytes=64)
            if r == 0:
                nc.vector.tensor_copy(picked[:], scores[r][:].indirect(column_list[:]))
            else:
                nc.scalar.activation(picked[:], scores[r][:].indirect(column_list[:]), ACT.Copy)
            inv_mean = pool.tile([P, 1], F32, name="inv_mean%d" % r)
            nc.vector.reciprocal(inv_mean[:], means[r][:])
            looked_up.append(picked)
            inv_means.append(inv_mean)

        for r, queue in enumerate((nc.scalar, nc.sync)):
            result = pool.tile([P, M], F32, name="result%d" % r, align_bytes=64)
            nc.vector.scalar_tensor_tensor(
                result[:], looked_up[r][:], inv_means[r][:], half_resid[:, r, :], ALU.mult, ALU.add
            )
            queue.dma_start(out[r * P : (r + 1) * P, :], result[:])
